import numpy as np
import ml_dtypes


def mxq(x, axis, fmt="e4m3"):
    dtype, down = {"e4m3": (ml_dtypes.float8_e4m3fn, 7), "e5m2": (ml_dtypes.float8_e5m2, 14)}[fmt]
    v = np.moveaxis(np.asarray(x, np.float32).astype(ml_dtypes.bfloat16).astype(np.float64), axis, -1)
    blocks = v.reshape(v.shape[:-1] + (-1, 32))
    amax = np.abs(blocks).max(-1, keepdims=True)
    byte = np.maximum(np.where(amax > 0, np.frexp(amax)[1] - 1 + 127, 0) - down, 1)
    scale = np.exp2(byte - 127.0)
    codes = (blocks / scale).astype(np.float32).astype(dtype).astype(np.float64)
    return np.moveaxis((codes * scale).reshape(v.shape), -1, axis)


WIDE = False


def mx_kscale(k):
    if not WIDE:
        return np.ones(k)
    levels = np.array([10, -10, 5, -5, 0])
    if k % 512:
        return np.exp2(np.random.permutation(np.resize(levels, k // 32))).repeat(32)
    a = np.empty((k // 512, 16))
    for p in range(k // 512):
        a[p, :8] = np.random.permutation(np.resize(levels, 8))
        for g in range(8):
            far = levels[np.abs(levels - a[p, g]) >= 10]
            a[p, g + 8] = far[np.random.randint(len(far))]
    return np.exp2(a.ravel()).repeat(32)


BF16 = ml_dtypes.bfloat16


def bf(x):
    return np.asarray(x, np.float32).astype(BF16)


def f64(x):
    return np.asarray(x).astype(np.float64)


E2M1 = np.array([0.0, 0.5, 1.0, 1.5, 2.0, 3.0, 4.0, 6.0, -0.0, -0.5, -1.0, -1.5, -2.0, -3.0, -4.0, -6.0])


def pack_weight(w, fmt):
    k, n = w.shape
    w = f64(bf(w)).reshape(k // 32, 32, n)
    amax = np.abs(w).max(1)
    if fmt == "e4m3":
        byte = np.frexp(amax)[1] - 1 + 127 - 7
    else:
        mant, ex = np.frexp(amax / 6.0)
        byte = np.where(mant > 0.5, ex, ex - 1) + 127
    byte = np.clip(np.where(amax > 0, byte, 1), 1, 254)
    scaled = (w * np.exp2(127.0 - byte)[:, None, :]).reshape(k, n).astype(np.float32)
    by_word = np.ascontiguousarray(scaled.reshape(k // 512, 128, 4, n).transpose(0, 1, 3, 2))
    if fmt == "e4m3":
        words = by_word.astype(ml_dtypes.float8_e4m3fn).view(np.uint8)
    else:
        c = by_word.astype(ml_dtypes.float4_e2m1fn).view(np.uint8) & 0xF
        words = c[..., 0::2] | (c[..., 1::2] << 4)
    return np.ascontiguousarray(words), np.ascontiguousarray(byte.astype(np.uint8).reshape(k // 512, 16, n))


def unpack_weight(words, scales, fmt):
    g, p, n, _ = words.shape
    if fmt == "e4m3":
        vals = np.ascontiguousarray(words).view(ml_dtypes.float8_e4m3fn).astype(np.float64)
    else:
        nib = np.empty((g, p, n, 4), np.uint8)
        nib[..., 0::2] = words & 0xF
        nib[..., 1::2] = words >> 4
        vals = E2M1[nib]
    vals = vals * np.repeat(np.exp2(scales.astype(np.float64) - 127.0), 8, axis=1)[..., None]
    return vals.transpose(0, 1, 3, 2).reshape(g * 512, n)
def pack4(w):
    words, scales = pack_weight(w, "e2m1")
    return words.reshape(words.shape[0], 128, -1), scales


def unpack4(words, scales):
    return unpack_weight(words.reshape(words.shape[0], 128, -1, 2), scales, "e2m1")


def planes(Y):
    n, m = Y.shape
    b = f64(bf(Y)).reshape(n // 32, 32, m)
    amax = np.abs(b).max(1)
    byte = np.clip(np.where(amax > 0, np.frexp(amax)[1] - 1 + 127 - 7, 1), 1, 254)
    codes = (b * np.exp2(127.0 - byte)[:, None, :]).reshape(n, m).astype(np.float32).astype(ml_dtypes.float8_e4m3fn).view(np.uint8)
    words = codes.reshape(n // 512, 128, 4, m).transpose(0, 1, 3, 2)
    return np.ascontiguousarray(words), np.ascontiguousarray(byte.astype(np.uint8).reshape(n // 512, 16, m))


S, V, K, N = 12, 128, 2048, 1024
LO, HI = K // 16, 3 * K // 16

def bandpass_matrix():
    H = np.zeros(K // 2 + 1, complex)
    H[LO:HI] = np.exp(2j * np.pi * np.random.rand(HI - LO))
    h = np.fft.irfft(H, K)
    h = h / np.sqrt(np.sum(h ** 2))
    lag = ((K // N) * np.arange(N)[None, :] - np.arange(K)[:, None]) % K
    return h[lag]

def setup_inputs():
    s = mx_kscale(K)
    w_words, w_scales = pack4(bandpass_matrix() / s[:, None])
    return {
        "x": bf(np.random.randn(S, V, K) * s),
        "w_words": w_words, "w_scales": w_scales,
        "c": bf(np.exp(0.3 * np.random.randn(S, V))),
        "d": bf(0.4 * np.random.randn(S, N)),
        "e": bf(np.exp(0.8 * np.random.randn(N))),
    }

def reference(x, w_words, w_scales, c, d, e):
    X = mxq(f64(x).reshape(S * V, K), 1, "e4m3")
    W = unpack4(w_words, w_scales)
    R = (X @ W).reshape(S, V, N)
    y = f64(e) * np.abs(f64(c)[:, :, None] * R - f64(d)[:, None, :])
    Y = y.reshape(S * V, N).T
    words, scales = planes(Y)
    return y, words, scales

@@ -1,0 +1,288 @@
+from contextlib import ExitStack
+
+import concourse.mybir as mybir
+from concourse.masks import make_identity
+
+S, V, K, N = 12, 128, 2048, 1024
+M = S * V
+FLOPS = 2 * M * K * N
+
+F32 = mybir.dt.float32
+BF16 = mybir.dt.bfloat16
+I32 = mybir.dt.int32
+U32 = mybir.dt.uint32
+U8 = mybir.dt.uint8
+FP8X4 = mybir.dt.float8_e4m3fn_x4
+FP4X4 = mybir.dt.float4_e2m1fn_x4
+ALU = mybir.AluOpType
+ACT = mybir.ActivationFunctionType
+
+P = 128
+PASSES = K // 512
+HALF = 512
+GROUP = 4
+GROUPS = S // GROUP
+TILES = S
+GROUP_ROWS = GROUP * P
+E_ROW = S
+
+
+def tile_bandpass_rectified_vibration_g4_kernel(tc, x, w_words, w_scales, c, d, e, out_0, out_1, out_2):
+    nc = tc.nc
+    x_rows = x.rearrange("a v k -> (a v) k").rearrange("(q p w) k -> q w p k", p=P, w=GROUP)
+    y_rows = out_0.rearrange("a v n -> (a v) n").rearrange("(q p w) n -> q w p n", p=P, w=GROUP)
+    c_cols = c.rearrange("a v -> (a v)").rearrange("(q p w) -> p q w", p=P, w=GROUP)
+    w_words32 = w_words.bitcast(I32)
+    w_scales32 = w_scales.bitcast(I32)
+    y_words32 = out_1.rearrange("g p m t -> g p (m t)").bitcast(I32).rearrange("g p m -> p g m")
+    y_scales32 = out_2.bitcast(I32)
+
+    with ExitStack() as ctx:
+        keep = ctx.enter_context(tc.tile_pool(name="keep", bufs=1))
+        work = ctx.enter_context(tc.tile_pool(name="work", bufs=3))
+        psum = ctx.enter_context(tc.psum_pool(name="psum", bufs=2))
+        ctx.enter_context(tc.manual_schedule())
+
+        ident = keep.tile([P, P], F32)
+        select = keep.tile([P, GROUPS + 1, P], BF16)
+        rows = keep.tile([P, N], BF16)
+        spread = [keep.tile([P, N], BF16, name="spread%d" % q) for q in range(GROUPS + 1)]
+        c_sb = keep.tile([P, GROUPS, GROUP], BF16)
+        w_sb = [keep.tile([P, 2 * N], U8, name="w%d" % g, align_bytes=64) for g in range(PASSES)]
+        w_plane = keep.tile([P, PASSES, N], U8, align_bytes=64)
+        warm = keep.tile([P, 8], F32)
+        warm_out = keep.tile([P, 8], F32)
+        x_first = [keep.tile([P, K // 2], BF16, name="x0_%d" % b) for b in range(2)]
+        x_rest = [keep.tile([P, K], BF16, name="x%d" % i) for i in range(1, TILES)]
+
+        def x_half(i, b):
+            if i == 0:
+                return x_first[b][:]
+            return x_rest[i - 1][:, b * (K // 2) : (b + 1) * (K // 2)]
+
+        def load_x(i):
+            nc.sync.dma_start(out=x_rest[i - 1][:], in_=x_rows[i // GROUP, i % GROUP])
+
+        def load_w(g):
+            nc.sync.dma_start(out=w_sb[g][:].bitcast(I32), in_=w_words32[g])
+
+        nc.vector.memset(w_plane[:].rearrange("p g n -> p (g n)").bitcast(I32), 0)
+        nc.vector.memset(rows[:].bitcast(I32), 0)
+        nc.vector.memset(warm[:], 0.0)
+        make_identity(nc, ident[:])
+        for b in range(2):
+            nc.sync.dma_start(out=x_first[b][:], in_=x_rows[0, 0][:, b * (K // 2) : (b + 1) * (K // 2)])
+        for quad in range(4):
+            nc.sync.dma_start(
+                out=w_plane[32 * quad : 32 * quad + 4, :, :].bitcast(I32),
+                in_=w_scales32[:, 4 * quad : 4 * quad + 4, :].rearrange("g r n -> r g n"),
+            )
+        nc.scalar.dma_start(out=rows[E_ROW : E_ROW + 1, :], in_=e.rearrange("(o n) -> o n", o=1))
+        nc.scalar.dma_start(out=rows[0:S, :], in_=d)
+        nc.scalar.dma_start(out=c_sb[:], in_=c_cols)
+        nc.scalar.activation(out=warm_out[:], in_=warm[:], func=ACT.Abs)
+        load_w(0)
+        load_w(1)
+        load_x(1)
+        load_w(2)
+        load_w(3)
+        for i in range(2, TILES):
+            load_x(i)
+        nc.vector.tensor_copy(
+            out=select[:, 0:GROUPS, :].rearrange("k q (a j) -> k (q a) j", a=GROUP),
+            in_=ident[:, 0:S].unsqueeze(2).to_broadcast([P, S, P // GROUP]),
+        )
+        nc.vector.tensor_copy(out=select[:, GROUPS, :], in_=ident[:, E_ROW : E_ROW + 1].to_broadcast([P, P]))
+
+        xt_bank, x_grouped, x_codes, x_plane = {}, {}, {}, {}
+        acc, z, mag, y, y_bf, yt_bank = {}, {}, {}, {}, {}, {}
+        y_grouped, y_codes, y_plane, spread_bank = {}, {}, {}, {}
+
+        def spread_matmul(q):
+            spread_bank[q] = psum.tile([P, N], BF16, name="yt", tag="yt")
+            for h in range(2):
+                cols = slice(h * HALF, (h + 1) * HALF)
+                nc.tensor.matmul(spread_bank[q][:, cols], lhsT=select[:, q, :], rhs=rows[:, cols], start=True, stop=True)
+
+        def transpose_x(i):
+            for b in range(2):
+                xt_bank[i, b] = psum.tile([P, 2, 2, P], F32, name="xt", tag="xt")
+                words = x_half(i, b).bitcast(F32)
+                for gl in range(2):
+                    for u in range(2):
+                        nc.tensor.transpose(xt_bank[i, b][:, gl, u, :], words[:, 256 * gl + u : 256 * (gl + 1) : 2], ident[:])
+
+        def copy_x(i, b, engine_copy):
+            x_grouped[i, b] = work.tile([P, K // 2], BF16, name="xg", tag="xg", bufs=4, align_bytes=64)
+            engine_copy(
+                out=x_grouped[i, b][:].bitcast(F32).rearrange("p (g r u) -> p g r u", g=2, u=2),
+                in_=xt_bank[i, b][:].rearrange("p g u r -> p g r u"),
+            )
+
+        def quantise_x(i, b):
+            x_codes[i, b] = work.tile([P, 2 * P], U32, name="xc", tag="xc", bufs=6, align_bytes=64)
+            x_plane[i, b] = work.tile([P, 2 * P], U8, name="xs", tag="xs", bufs=6, align_bytes=64)
+            nc.vector.quantize_mx(out=x_codes[i, b][:].bitcast(FP8X4), scales=x_plane[i, b][:], in_=x_grouped[i, b][:])
+
+        def mx_pass(i, h, g):
+            if g == 0:
+                acc[i, h] = psum.tile([P, HALF], F32, name="acc", tag="acc", bufs=4)
+            cols = slice((g % 2) * P, (g % 2 + 1) * P)
+            nc.tensor.matmul_mx(
+                out=acc[i, h][:],
+                lhsT=x_codes[i, g // 2][:, cols].bitcast(FP8X4),
+                lhsT_scale=x_plane[i, g // 2][:, cols],
+                rhs=w_sb[g][:, 2 * h * HALF : 2 * (h + 1) * HALF].bitcast(FP4X4),
+                rhs_scale=w_plane[:, g, h * HALF : (h + 1) * HALF],
+                start=(g == 0),
+                stop=(g == PASSES - 1),
+            )
+
+        def calibrate(i, h):
+            z[i, h] = work.tile([P, HALF], F32, name="z", tag="z")
+            q, w = divmod(i, GROUP)
+            nc.vector.scalar_tensor_tensor(
+                out=z[i, h][:],
+                in0=acc[i, h][:],
+                scalar=c_sb[:, q, w : w + 1],
+                in1=spread[q][:, h * HALF : (h + 1) * HALF],
+                op0=ALU.mult,
+                op1=ALU.subtract,
+            )
+
+        def rectify(i, h):
+            mag[i, h] = work.tile([P, HALF], F32, name="mag", tag="mag")
+            nc.scalar.activation(out=mag[i, h][:], in_=z[i, h][:], func=ACT.Abs)
+
+        def weigh(i, h):
+            if h == 0:
+                y[i] = work.tile([P, N], F32, name="y", tag="y", bufs=6)
+            cols = slice(h * HALF, (h + 1) * HALF)
+            nc.vector.tensor_tensor(out=y[i][:, cols], in0=mag[i, h][:], in1=spread[GROUPS][:, cols], op=ALU.mult)
+
+        def store_y(i, cols):
+            nc.sync.dma_start(out=y_rows[i // GROUP, i % GROUP][:, cols], in_=y[i][:, cols])
+
+        def round_y(i, h, engine_copy):
+            y_bf[i, h] = work.tile([P, HALF], BF16, name="ybf", tag="ybf", bufs=8)
+            engine_copy(
+                out=y_bf[i, h][:].rearrange("r (u p e) -> r u p e", u=2, e=2),
+                in_=y[i][:, h * HALF : (h + 1) * HALF].rearrange("r (p u e) -> r u p e", u=2, e=2),
+            )
+
+        def transpose_y(pair, h):
+            yt_bank[pair, h] = psum.tile([P, 2, 2, P], F32, name="yt", tag="yt")
+            for wl in range(2):
+                words = y_bf[2 * pair + wl, h][:].bitcast(F32)
+                for u in range(2):
+                    nc.tensor.transpose(yt_bank[pair, h][:, wl, u, :], words[:, u * P : (u + 1) * P], ident[:])
+
+        def copy_y(pair, h, engine_copy):
+            q, wp = divmod(pair, 2)
+            if wp == 0:
+                y_grouped[q, h] = work.tile([P, 4 * GROUP_ROWS], BF16, name="yg", tag="yg", bufs=4, align_bytes=64)
+            engine_copy(
+                out=y_grouped[q, h][:].bitcast(F32).rearrange("p (r a s) -> p r a s", a=2, s=4)[:, :, wp, :],
+                in_=yt_bank[pair, h][:].rearrange("p w u r -> p r (w u)"),
+            )
+
+        def quantise_y(q, h):
+            y_codes[q, h] = keep.tile([P, GROUP_ROWS], U32, name="yc%d_%d" % (q, h), align_bytes=64)
+            if h == 0:
+                y_plane[q] = keep.tile([P, 2, GROUP_ROWS], U8, name="ys%d" % q, align_bytes=64)
+            nc.vector.quantize_mx(out=y_codes[q, h][:].bitcast(FP8X4), scales=y_plane[q][:, h, :], in_=y_grouped[q, h][:])
+
+        def store_codes(q, h):
+            nc.sync.dma_start(
+                out=y_words32[:, h, q * GROUP_ROWS : (q + 1) * GROUP_ROWS], in_=y_codes[q, h][:].bitcast(I32)
+            )
+
+        def store_scales(q):
+            width = GROUP_ROWS // 4
+            for quad in range(4):
+                nc.sync.dma_start(
+                    out=y_scales32[:, 4 * quad : 4 * quad + 4, q * width : (q + 1) * width].rearrange("g r m -> r g m"),
+                    in_=y_plane[q][32 * quad : 32 * quad + 4, :, :].bitcast(I32),
+                )
+
+        vcopy = nc.vector.tensor_copy
+        scopy = nc.scalar.copy
+
+        transpose_x(0)
+        copy_x(0, 0, scopy)
+        copy_x(0, 1, vcopy)
+        quantise_x(0, 0)
+        spread_matmul(GROUPS)
+        spread_matmul(0)
+        scopy(out=spread[GROUPS][:], in_=spread_bank[GROUPS][:])
+        quantise_x(0, 1)
+        vcopy(out=spread[0][:], in_=spread_bank[0][:])
+
+        last = TILES - 1
+        for i in range(TILES):
+            nxt, prev = i + 1, i - 1
+            if nxt <= last:
+                transpose_x(nxt)
+            if prev >= 0:
+                calibrate(prev, 1)
+                weigh(prev, 0)
+            if nxt <= last:
+                copy_x(nxt, 0, scopy)
+            if prev >= 0:
+                rectify(prev, 1)
+            if nxt <= last:
+                copy_x(nxt, 1, scopy)
+                quantise_x(nxt, 0)
+            if prev >= 0:
+                round_y(prev, 0, vcopy)
+                weigh(prev, 1)
+                store_y(prev, slice(0, N))
+            if nxt <= last:
+                quantise_x(nxt, 1)
+            if 1 <= i < GROUPS:
+                spread_matmul(i)
+                scopy(out=spread[i][:], in_=spread_bank[i][:])
+            pair = (i - 3) // 2
+            if i >= 3 and i % 2 == 1:
+                transpose_y(pair, 0)
+                transpose_y(pair, 1)
+            if i >= 3:
+                copy_y(pair, (i - 3) % 2, scopy)
+            if i == last:
+                copy_y(pair, 1, scopy)
+            if prev >= 0:
+                round_y(prev, 1, scopy)
+            if i == 0:
+                for g in range(PASSES):
+                    for h in range(2):
+                        mx_pass(i, h, g)
+            else:
+                for h in range(2):
+                    for g in range(PASSES):
+                        mx_pass(i, h, g)
+            calibrate(i, 0)
+            rectify(i, 0)
+            if i >= 3 and pair % 2 == 1:
+                quantise_y(pair // 2, (i - 3) % 2)
+                store_codes(pair // 2, (i - 3) % 2)
+                if (i - 3) % 2 == 1:
+                    store_scales(pair // 2)
+
+        pair, q = last // 2, GROUPS - 1
+        calibrate(last, 1)
+        weigh(last, 0)
+        rectify(last, 1)
+        store_y(last, slice(0, HALF))
+        round_y(last, 0, scopy)
+        weigh(last, 1)
+        store_y(last, slice(HALF, N))
+        transpose_y(pair, 0)
+        round_y(last, 1, vcopy)
+        copy_y(pair, 0, scopy)
+        transpose_y(pair, 1)
+        quantise_y(q, 0)
+        store_codes(q, 0)
+        copy_y(pair, 1, scopy)
+        quantise_y(q, 1)
+        store_codes(q, 1)
+        store_scales(q)

@@ -20,19 +20,30 @@ ACT = mybir.ActivationFunctionType
 P = 128
 PASSES = K // 512
 HALF = 512
-GROUP = 4
-GROUPS = S // GROUP
+GROUP_SIZES = [4, 4, 2, 1, 1]
 TILES = S
-GROUP_ROWS = GROUP * P
-E_ROW = S
+WARM_MATMULS = 4
+CODE_STORES = [[0], [1], [2, 3], [4]]
+SCALE_STORES = [[0, 1], [2, 3, 4]]
 
 
 def tile_bandpass_rectified_vibration_g4_kernel(tc, x, w_words, w_scales, c, d, e, out_0, out_1, out_2):
     nc = tc.nc
-    x_rows = x.rearrange("a v k -> (a v) k").rearrange("(q p w) k -> q w p k", p=P, w=GROUP)
-    y_rows = out_0.rearrange("a v n -> (a v) n").rearrange("(q p w) n -> q w p n", p=P, w=GROUP)
-    c_cols = c.rearrange("a v -> (a v)").rearrange("(q p w) -> p q w", p=P, w=GROUP)
-    w_words32 = w_words.bitcast(I32)
+    x_flat = x.rearrange("a v k -> (a v) k")
+    y_flat = out_0.rearrange("a v n -> (a v) n")
+    c_flat = c.rearrange("a v -> (a v)")
+    first_tile = [sum(GROUP_SIZES[:q]) for q in range(len(GROUP_SIZES))]
+    place = [(q, w) for q, size in enumerate(GROUP_SIZES) for w in range(size)]
+    units = [(q, w, min(2, size)) for q, size in enumerate(GROUP_SIZES) for w in range(0, size, 2)]
+
+    def group_span(q):
+        return slice(first_tile[q] * P, (first_tile[q] + GROUP_SIZES[q]) * P)
+
+    def tile_rows(flat, i):
+        q, w = place[i]
+        return flat[group_span(q), :].rearrange("(p w) n -> w p n", p=P)[w]
+
+    w_words32 = w_words.bitcast(I32).rearrange("g p n -> p g n")
     w_scales32 = w_scales.bitcast(I32)
     y_words32 = out_1.rearrange("g p m t -> g p (m t)").bitcast(I32).rearrange("g p m -> p g m")
     y_scales32 = out_2.bitcast(I32)
@@ -44,13 +55,25 @@ def tile_bandpass_rectified_vibration_g4_kernel(tc, x, w_words, w_scales, c, d, 
         ctx.enter_context(tc.manual_schedule())
 
         ident = keep.tile([P, P], F32)
-        select = keep.tile([P, GROUPS + 1, P], BF16)
+        select = keep.tile([P, 2, P], BF16)
         rows = keep.tile([P, N], BF16)
-        spread = [keep.tile([P, N], BF16, name="spread%d" % q) for q in range(GROUPS + 1)]
-        c_sb = keep.tile([P, GROUPS, GROUP], BF16)
-        w_sb = [keep.tile([P, 2 * N], U8, name="w%d" % g, align_bytes=64) for g in range(PASSES)]
+        d_sb = [keep.tile([P, N], BF16, name="d%d" % q) for q in range(len(GROUP_SIZES))]
+        e_sb = keep.tile([P, N], BF16)
+        c_sb = [keep.tile([P, size], BF16, name="c%d" % q) for q, size in enumerate(GROUP_SIZES)]
+        w_sb = [keep.tile([P, 2, 2 * N], U8, name="w%d" % b, align_bytes=64) for b in range(2)]
         w_plane = keep.tile([P, PASSES, N], U8, align_bytes=64)
-        warm = keep.tile([P, 8], F32)
+        code_batch, scale_batch = {}, {}
+        for n, members in enumerate(CODE_STORES):
+            span = slice(group_span(members[0]).start, group_span(members[-1]).stop)
+            codes = keep.tile([P, 2, span.stop - span.start], U32, name="yc%d" % n, align_bytes=64)
+            for q in members:
+                code_batch[q] = (codes, span, q == members[-1])
+        for n, members in enumerate(SCALE_STORES):
+            span = slice(group_span(members[0]).start, group_span(members[-1]).stop)
+            plane = keep.tile([P, 2, span.stop - span.start], U8, name="ys%d" % n, align_bytes=64)
+            for q in members:
+                scale_batch[q] = (plane, span, q == members[-1])
+        warm = keep.tile([P, HALF], BF16)
         warm_out = keep.tile([P, 8], F32)
         x_first = [keep.tile([P, K // 2], BF16, name="x0_%d" % b) for b in range(2)]
         x_rest = [keep.tile([P, K], BF16, name="x%d" % i) for i in range(1, TILES)]
@@ -61,42 +84,57 @@ def tile_bandpass_rectified_vibration_g4_kernel(tc, x, w_words, w_scales, c, d, 
             return x_rest[i - 1][:, b * (K // 2) : (b + 1) * (K // 2)]
 
         def load_x(i):
-            nc.sync.dma_start(out=x_rest[i - 1][:], in_=x_rows[i // GROUP, i % GROUP])
+            nc.sync.dma_start(out=x_rest[i - 1][:], in_=tile_rows(x_flat, i))
 
-        def load_w(g):
-            nc.sync.dma_start(out=w_sb[g][:].bitcast(I32), in_=w_words32[g])
+        def load_w(b):
+            nc.sync.dma_start(out=w_sb[b][:].bitcast(I32), in_=w_words32[:, 2 * b : 2 * b + 2, :])
 
-        nc.vector.memset(w_plane[:].rearrange("p g n -> p (g n)").bitcast(I32), 0)
+        def load_c(q):
+            nc.sync.dma_start(out=c_sb[q][:], in_=c_flat[group_span(q)].rearrange("(p w) -> p w", p=P))
+
+        def load_d(q):
+            share = P // GROUP_SIZES[q]
+            for a in range(GROUP_SIZES[q]):
+                nc.sync.dma_start(
+                    out=d_sb[q][a * share : (a + 1) * share, :], in_=d[first_tile[q] + a].partition_broadcast(share)
+                )
+
+        size0 = GROUP_SIZES[0]
+        nc.vector.memset(warm[:].bitcast(I32), 0)
         nc.vector.memset(rows[:].bitcast(I32), 0)
-        nc.vector.memset(warm[:], 0.0)
+        nc.vector.memset(w_plane[:].rearrange("p g n -> p (g n)").bitcast(I32), 0)
         make_identity(nc, ident[:])
+        nc.scalar.activation(out=warm_out[:], in_=warm[:, 0:8], func=ACT.Abs)
         for b in range(2):
-            nc.sync.dma_start(out=x_first[b][:], in_=x_rows[0, 0][:, b * (K // 2) : (b + 1) * (K // 2)])
+            nc.sync.dma_start(out=x_first[b][:], in_=tile_rows(x_flat, 0)[:, b * (K // 2) : (b + 1) * (K // 2)])
+        nc.sync.dma_start(out=rows[0:size0, :], in_=d[0:size0, :])
+        nc.sync.dma_start(out=rows[size0 : size0 + 1, :], in_=e.rearrange("(o n) -> o n", o=1))
+        load_w(0)
         for quad in range(4):
             nc.sync.dma_start(
                 out=w_plane[32 * quad : 32 * quad + 4, :, :].bitcast(I32),
                 in_=w_scales32[:, 4 * quad : 4 * quad + 4, :].rearrange("g r n -> r g n"),
             )
-        nc.scalar.dma_start(out=rows[E_ROW : E_ROW + 1, :], in_=e.rearrange("(o n) -> o n", o=1))
-        nc.scalar.dma_start(out=rows[0:S, :], in_=d)
-        nc.scalar.dma_start(out=c_sb[:], in_=c_cols)
-        nc.scalar.activation(out=warm_out[:], in_=warm[:], func=ACT.Abs)
-        load_w(0)
-        load_w(1)
         load_x(1)
-        load_w(2)
-        load_w(3)
+        load_w(1)
+        load_c(0)
         for i in range(2, TILES):
             load_x(i)
+            if i + 1 in first_tile:
+                load_c(place[i + 1][0])
+                load_d(place[i + 1][0])
         nc.vector.tensor_copy(
-            out=select[:, 0:GROUPS, :].rearrange("k q (a j) -> k (q a) j", a=GROUP),
-            in_=ident[:, 0:S].unsqueeze(2).to_broadcast([P, S, P // GROUP]),
+            out=select[:, 0, :].rearrange("k (a j) -> k a j", a=size0),
+            in_=ident[:, 0:size0].unsqueeze(2).to_broadcast([P, size0, P // size0]),
         )
-        nc.vector.tensor_copy(out=select[:, GROUPS, :], in_=ident[:, E_ROW : E_ROW + 1].to_broadcast([P, P]))
+        nc.vector.tensor_copy(out=select[:, 1, :], in_=ident[:, size0 : size0 + 1].to_broadcast([P, P]))
+        warm_bank = psum.tile([P, HALF], F32, name="acc", tag="acc", bufs=4)
+        for j in range(WARM_MATMULS):
+            nc.tensor.matmul(warm_bank[:], lhsT=warm[:, 0:P], rhs=warm[:], start=True, stop=True)
 
         xt_bank, x_grouped, x_codes, x_plane = {}, {}, {}, {}
         acc, z, mag, y, y_bf, yt_bank = {}, {}, {}, {}, {}, {}
-        y_grouped, y_codes, y_plane, spread_bank = {}, {}, {}, {}
+        y_grouped, spread_bank = {}, {}
 
         def spread_matmul(q):
             spread_bank[q] = psum.tile([P, N], BF16, name="yt", tag="yt")
@@ -132,78 +170,85 @@ def tile_bandpass_rectified_vibration_g4_kernel(tc, x, w_words, w_scales, c, d, 
                 out=acc[i, h][:],
                 lhsT=x_codes[i, g // 2][:, cols].bitcast(FP8X4),
                 lhsT_scale=x_plane[i, g // 2][:, cols],
-                rhs=w_sb[g][:, 2 * h * HALF : 2 * (h + 1) * HALF].bitcast(FP4X4),
+                rhs=w_sb[g // 2][:, g % 2, 2 * h * HALF : 2 * (h + 1) * HALF].bitcast(FP4X4),
                 rhs_scale=w_plane[:, g, h * HALF : (h + 1) * HALF],
                 start=(g == 0),
                 stop=(g == PASSES - 1),
             )
 
-        def calibrate(i, h):
-            z[i, h] = work.tile([P, HALF], F32, name="z", tag="z")
-            q, w = divmod(i, GROUP)
+        def calibrate(i, h, part=slice(0, HALF)):
+            if part.start == 0:
+                z[i, h] = work.tile([P, HALF], F32, name="z", tag="z")
+            q, w = place[i]
             nc.vector.scalar_tensor_tensor(
-                out=z[i, h][:],
-                in0=acc[i, h][:],
-                scalar=c_sb[:, q, w : w + 1],
-                in1=spread[q][:, h * HALF : (h + 1) * HALF],
+                out=z[i, h][:, part],
+                in0=acc[i, h][:, part],
+                scalar=c_sb[q][:, w : w + 1],
+                in1=d_sb[q][:, h * HALF + part.start : h * HALF + part.stop],
                 op0=ALU.mult,
                 op1=ALU.subtract,
             )
 
-        def rectify(i, h):
-            mag[i, h] = work.tile([P, HALF], F32, name="mag", tag="mag")
-            nc.scalar.activation(out=mag[i, h][:], in_=z[i, h][:], func=ACT.Abs)
+        def rectify(i, h, part=slice(0, HALF)):
+            if part.start == 0:
+                mag[i, h] = work.tile([P, HALF], F32, name="mag", tag="mag")
+            nc.scalar.activation(out=mag[i, h][:, part], in_=z[i, h][:, part], func=ACT.Abs)
 
-        def weigh(i, h):
-            if h == 0:
+        def weigh(i, h, part=slice(0, HALF)):
+            if h == 0 and part.start == 0:
                 y[i] = work.tile([P, N], F32, name="y", tag="y", bufs=6)
-            cols = slice(h * HALF, (h + 1) * HALF)
-            nc.vector.tensor_tensor(out=y[i][:, cols], in0=mag[i, h][:], in1=spread[GROUPS][:, cols], op=ALU.mult)
+            cols = slice(h * HALF + part.start, h * HALF + part.stop)
+            nc.vector.tensor_tensor(out=y[i][:, cols], in0=mag[i, h][:, part], in1=e_sb[:, cols], op=ALU.mult)
 
         def store_y(i, cols):
-            nc.sync.dma_start(out=y_rows[i // GROUP, i % GROUP][:, cols], in_=y[i][:, cols])
+            nc.sync.dma_start(out=tile_rows(y_flat, i)[:, cols], in_=y[i][:, cols])
 
-        def round_y(i, h, engine_copy):
-            y_bf[i, h] = work.tile([P, HALF], BF16, name="ybf", tag="ybf", bufs=8)
+        def round_y(i, h, engine_copy, part=slice(0, HALF)):
+            if part.start == 0:
+                y_bf[i, h] = work.tile([P, HALF], BF16, name="ybf", tag="ybf", bufs=8)
             engine_copy(
-                out=y_bf[i, h][:].rearrange("r (u p e) -> r u p e", u=2, e=2),
-                in_=y[i][:, h * HALF : (h + 1) * HALF].rearrange("r (p u e) -> r u p e", u=2, e=2),
+                out=y_bf[i, h][:].rearrange("r (u p e) -> r u p e", u=2, e=2)[:, :, part.start // 4 : part.stop // 4, :],
+                in_=y[i][:, h * HALF + part.start : h * HALF + part.stop].rearrange("r (p u e) -> r u p e", u=2, e=2),
             )
 
-        def transpose_y(pair, h):
-            yt_bank[pair, h] = psum.tile([P, 2, 2, P], F32, name="yt", tag="yt")
-            for wl in range(2):
-                words = y_bf[2 * pair + wl, h][:].bitcast(F32)
+        def transpose_y(unit, h, tag):
+            q, w0, count = units[unit]
+            yt_bank[unit, h] = psum.tile([P, count, 2, P], F32, name=tag, tag=tag)
+            for wl in range(count):
+                words = y_bf[first_tile[q] + w0 + wl, h][:].bitcast(F32)
                 for u in range(2):
-                    nc.tensor.transpose(yt_bank[pair, h][:, wl, u, :], words[:, u * P : (u + 1) * P], ident[:])
+                    nc.tensor.transpose(yt_bank[unit, h][:, wl, u, :], words[:, u * P : (u + 1) * P], ident[:])
 
-        def copy_y(pair, h, engine_copy):
-            q, wp = divmod(pair, 2)
-            if wp == 0:
-                y_grouped[q, h] = work.tile([P, 4 * GROUP_ROWS], BF16, name="yg", tag="yg", bufs=4, align_bytes=64)
+        def copy_y(unit, h, engine_copy):
+            q, w0, count = units[unit]
+            size = GROUP_SIZES[q]
+            if w0 == 0:
+                y_grouped[q, h] = work.tile([P, 4 * size * P], BF16, name="yg", tag="yg", bufs=4, align_bytes=64)
             engine_copy(
-                out=y_grouped[q, h][:].bitcast(F32).rearrange("p (r a s) -> p r a s", a=2, s=4)[:, :, wp, :],
-                in_=yt_bank[pair, h][:].rearrange("p w u r -> p r (w u)"),
+                out=y_grouped[q, h][:].bitcast(F32).rearrange("p (r s) -> p r s", r=P)[:, :, 2 * w0 : 2 * (w0 + count)],
+                in_=yt_bank[unit, h][:].rearrange("p w u r -> p r (w u)"),
             )
 
         def quantise_y(q, h):
-            y_codes[q, h] = keep.tile([P, GROUP_ROWS], U32, name="yc%d_%d" % (q, h), align_bytes=64)
-            if h == 0:
-                y_plane[q] = keep.tile([P, 2, GROUP_ROWS], U8, name="ys%d" % q, align_bytes=64)
-            nc.vector.quantize_mx(out=y_codes[q, h][:].bitcast(FP8X4), scales=y_plane[q][:, h, :], in_=y_grouped[q, h][:])
-
-        def store_codes(q, h):
-            nc.sync.dma_start(
-                out=y_words32[:, h, q * GROUP_ROWS : (q + 1) * GROUP_ROWS], in_=y_codes[q, h][:].bitcast(I32)
+            codes, code_span, codes_done = code_batch[q]
+            plane, scale_span, scales_done = scale_batch[q]
+            own = group_span(q)
+            nc.vector.quantize_mx(
+                out=codes[:, h, own.start - code_span.start : own.stop - code_span.start].bitcast(FP8X4),
+                scales=plane[:, h, own.start - scale_span.start : own.stop - scale_span.start],
+                in_=y_grouped[q, h][:],
             )
-
-        def store_scales(q):
-            width = GROUP_ROWS // 4
-            for quad in range(4):
-                nc.sync.dma_start(
-                    out=y_scales32[:, 4 * quad : 4 * quad + 4, q * width : (q + 1) * width].rearrange("g r m -> r g m"),
-                    in_=y_plane[q][32 * quad : 32 * quad + 4, :, :].bitcast(I32),
-                )
+            if h == 1 and codes_done:
+                nc.sync.dma_start(out=y_words32[:, :, code_span], in_=codes[:].bitcast(I32))
+            if h == 1 and scales_done:
+                for quad in range(4):
+                    queue = nc.scalar if q == len(GROUP_SIZES) - 1 and quad % 2 == 0 else nc.sync
+                    queue.dma_start(
+                        out=y_scales32[:, 4 * quad : 4 * quad + 4, scale_span.start // 4 : scale_span.stop // 4].rearrange(
+                            "g r m -> r g m"
+                        ),
+                        in_=plane[32 * quad : 32 * quad + 4, :, :].bitcast(I32),
+                    )
 
         vcopy = nc.vector.tensor_copy
         scopy = nc.scalar.copy
@@ -212,13 +257,17 @@ def tile_bandpass_rectified_vibration_g4_kernel(tc, x, w_words, w_scales, c, d, 
         copy_x(0, 0, scopy)
         copy_x(0, 1, vcopy)
         quantise_x(0, 0)
-        spread_matmul(GROUPS)
         spread_matmul(0)
-        scopy(out=spread[GROUPS][:], in_=spread_bank[GROUPS][:])
+        spread_matmul(1)
+        scopy(out=d_sb[0][:], in_=spread_bank[0][:])
         quantise_x(0, 1)
-        vcopy(out=spread[0][:], in_=spread_bank[0][:])
+        vcopy(out=e_sb[:], in_=spread_bank[1][:])
+        for g in range(2):
+            for h in range(2):
+                mx_pass(0, h, g)
 
         last = TILES - 1
+        unit_at = {first_tile[q] + w0 + count + 1: n for n, (q, w0, count) in enumerate(units)}
         for i in range(TILES):
             nxt, prev = i + 1, i - 1
             if nxt <= last:
@@ -239,50 +288,61 @@ def tile_bandpass_rectified_vibration_g4_kernel(tc, x, w_words, w_scales, c, d, 
                 store_y(prev, slice(0, N))
             if nxt <= last:
                 quantise_x(nxt, 1)
-            if 1 <= i < GROUPS:
-                spread_matmul(i)
-                scopy(out=spread[i][:], in_=spread_bank[i][:])
-            pair = (i - 3) // 2
-            if i >= 3 and i % 2 == 1:
-                transpose_y(pair, 0)
-                transpose_y(pair, 1)
-            if i >= 3:
-                copy_y(pair, (i - 3) % 2, scopy)
-            if i == last:
-                copy_y(pair, 1, scopy)
+            copied = []
+            if i in unit_at:
+                transpose_y(unit_at[i], 0, "yt")
+                transpose_y(unit_at[i], 1, "yt")
+                copied = [(unit_at[i], 0)] + ([(unit_at[i], 1)] if i == last else [])
+            elif prev in unit_at:
+                copied = [(unit_at[prev], 1)]
+            for unit, h in copied:
+                copy_y(unit, h, scopy)
             if prev >= 0:
                 round_y(prev, 1, scopy)
             if i == 0:
-                for g in range(PASSES):
-                    for h in range(2):
+                for h in range(2):
+                    for g in range(2, PASSES):
                         mx_pass(i, h, g)
             else:
                 for h in range(2):
                     for g in range(PASSES):
                         mx_pass(i, h, g)
+            if i == last:
+                break
             calibrate(i, 0)
             rectify(i, 0)
-            if i >= 3 and pair % 2 == 1:
-                quantise_y(pair // 2, (i - 3) % 2)
-                store_codes(pair // 2, (i - 3) % 2)
-                if (i - 3) % 2 == 1:
-                    store_scales(pair // 2)
+            for unit, h in copied:
+                q, w0, count = units[unit]
+                if w0 + count == GROUP_SIZES[q]:
+                    quantise_y(q, h)
 
-        pair, q = last // 2, GROUPS - 1
-        calibrate(last, 1)
+        groups = len(GROUP_SIZES)
+        lo, hi = slice(0, HALF // 2), slice(HALF // 2, HALF)
+        calibrate(last, 0)
+        rectify(last, 0)
+        quantise_y(groups - 3, 0)
+        transpose_y(len(units) - 2, 0, "xt")
+        transpose_y(len(units) - 2, 1, "xt")
+        calibrate(last, 1, lo)
+        calibrate(last, 1, hi)
+        rectify(last, 1, lo)
+        rectify(last, 1, hi)
         weigh(last, 0)
-        rectify(last, 1)
         store_y(last, slice(0, HALF))
         round_y(last, 0, scopy)
-        weigh(last, 1)
+        weigh(last, 1, lo)
+        weigh(last, 1, hi)
         store_y(last, slice(HALF, N))
-        transpose_y(pair, 0)
-        round_y(last, 1, vcopy)
-        copy_y(pair, 0, scopy)
-        transpose_y(pair, 1)
-        quantise_y(q, 0)
-        store_codes(q, 0)
-        copy_y(pair, 1, scopy)
-        quantise_y(q, 1)
-        store_codes(q, 1)
-        store_scales(q)
+        round_y(last, 1, vcopy, lo)
+        round_y(last, 1, vcopy, hi)
+        transpose_y(len(units) - 1, 0, "yt")
+        transpose_y(len(units) - 1, 1, "yt")
+        copy_y(len(units) - 2, 0, scopy)
+        copy_y(len(units) - 2, 1, scopy)
+        quantise_y(groups - 3, 1)
+        quantise_y(groups - 2, 0)
+        quantise_y(groups - 2, 1)
+        copy_y(len(units) - 1, 0, scopy)
+        copy_y(len(units) - 1, 1, scopy)
+        quantise_y(groups - 1, 0)
+        quantise_y(groups - 1, 1)

@@ -20,11 +20,11 @@ ACT = mybir.ActivationFunctionType
 P = 128
 PASSES = K // 512
 HALF = 512
-GROUP_SIZES = [4, 4, 2, 1, 1]
+GROUP_SIZES = [4, 4, 4]
 TILES = S
 WARM_MATMULS = 4
-CODE_STORES = [[0], [1], [2, 3], [4]]
-SCALE_STORES = [[0, 1], [2, 3, 4]]
+CODE_STORES = [[0], [1], [2]]
+SCALE_STORES = [[0, 1], [2]]
 
 
 def tile_bandpass_rectified_vibration_g4_kernel(tc, x, w_words, w_scales, c, d, e, out_0, out_1, out_2):
@@ -55,7 +55,7 @@ def tile_bandpass_rectified_vibration_g4_kernel(tc, x, w_words, w_scales, c, d, 
         ctx.enter_context(tc.manual_schedule())
 
         ident = keep.tile([P, P], F32)
-        select = keep.tile([P, 2, P], BF16)
+        select = keep.tile([P, len(GROUP_SIZES) + 1, P], BF16)
         rows = keep.tile([P, N], BF16)
         d_sb = [keep.tile([P, N], BF16, name="d%d" % q) for q in range(len(GROUP_SIZES))]
         e_sb = keep.tile([P, N], BF16)
@@ -92,13 +92,6 @@ def tile_bandpass_rectified_vibration_g4_kernel(tc, x, w_words, w_scales, c, d, 
         def load_c(q):
             nc.sync.dma_start(out=c_sb[q][:], in_=c_flat[group_span(q)].rearrange("(p w) -> p w", p=P))
 
-        def load_d(q):
-            share = P // GROUP_SIZES[q]
-            for a in range(GROUP_SIZES[q]):
-                nc.sync.dma_start(
-                    out=d_sb[q][a * share : (a + 1) * share, :], in_=d[first_tile[q] + a].partition_broadcast(share)
-                )
-
         size0 = GROUP_SIZES[0]
         nc.vector.memset(warm[:].bitcast(I32), 0)
         nc.vector.memset(rows[:].bitcast(I32), 0)
@@ -107,8 +100,8 @@ def tile_bandpass_rectified_vibration_g4_kernel(tc, x, w_words, w_scales, c, d, 
         nc.scalar.activation(out=warm_out[:], in_=warm[:, 0:8], func=ACT.Abs)
         for b in range(2):
             nc.sync.dma_start(out=x_first[b][:], in_=tile_rows(x_flat, 0)[:, b * (K // 2) : (b + 1) * (K // 2)])
-        nc.sync.dma_start(out=rows[0:size0, :], in_=d[0:size0, :])
-        nc.sync.dma_start(out=rows[size0 : size0 + 1, :], in_=e.rearrange("(o n) -> o n", o=1))
+        nc.sync.dma_start(out=rows[0:S, :], in_=d)
+        nc.sync.dma_start(out=rows[S : S + 1, :], in_=e.rearrange("(o n) -> o n", o=1))
         load_w(0)
         for quad in range(4):
             nc.sync.dma_start(
@@ -122,12 +115,11 @@ def tile_bandpass_rectified_vibration_g4_kernel(tc, x, w_words, w_scales, c, d, 
             load_x(i)
             if i + 1 in first_tile:
                 load_c(place[i + 1][0])
-                load_d(place[i + 1][0])
         nc.vector.tensor_copy(
-            out=select[:, 0, :].rearrange("k (a j) -> k a j", a=size0),
-            in_=ident[:, 0:size0].unsqueeze(2).to_broadcast([P, size0, P // size0]),
+            out=select[:, 0:3, :].rearrange("k q (a j) -> k (q a) j", a=size0),
+            in_=ident[:, 0:S].unsqueeze(2).to_broadcast([P, S, P // size0]),
         )
-        nc.vector.tensor_copy(out=select[:, 1, :], in_=ident[:, size0 : size0 + 1].to_broadcast([P, P]))
+        nc.vector.tensor_copy(out=select[:, 3, :], in_=ident[:, S : S + 1].to_broadcast([P, P]))
         warm_bank = psum.tile([P, HALF], F32, name="acc", tag="acc", bufs=4)
         for j in range(WARM_MATMULS):
             nc.tensor.matmul(warm_bank[:], lhsT=warm[:, 0:P], rhs=warm[:], start=True, stop=True)
@@ -136,40 +128,47 @@ def tile_bandpass_rectified_vibration_g4_kernel(tc, x, w_words, w_scales, c, d, 
         acc, z, mag, y, y_bf, yt_bank = {}, {}, {}, {}, {}, {}
         y_grouped, spread_bank = {}, {}
 
-        def spread_matmul(q):
-            spread_bank[q] = psum.tile([P, N], BF16, name="yt", tag="yt")
+        def spread_matmul(q, tag, bufs):
+            spread_bank[q] = psum.tile([P, N], BF16, name=tag, tag=tag, bufs=bufs)
             for h in range(2):
                 cols = slice(h * HALF, (h + 1) * HALF)
                 nc.tensor.matmul(spread_bank[q][:, cols], lhsT=select[:, q, :], rhs=rows[:, cols], start=True, stop=True)
 
-        def transpose_x(i):
+        def transpose_x(i, tag="xt"):
             for b in range(2):
-                xt_bank[i, b] = psum.tile([P, 2, 2, P], F32, name="xt", tag="xt")
+                xt_bank[i, b] = psum.tile([P, 2, 2, P], F32, name=tag, tag=tag)
                 words = x_half(i, b).bitcast(F32)
                 for gl in range(2):
                     for u in range(2):
                         nc.tensor.transpose(xt_bank[i, b][:, gl, u, :], words[:, 256 * gl + u : 256 * (gl + 1) : 2], ident[:])
 
         def copy_x(i, b, engine_copy):
-            x_grouped[i, b] = work.tile([P, K // 2], BF16, name="xg", tag="xg", bufs=4, align_bytes=64)
+            if b == 0:
+                x_grouped[i] = work.tile([P, K], BF16, name="xg", tag="xg", align_bytes=64)
             engine_copy(
-                out=x_grouped[i, b][:].bitcast(F32).rearrange("p (g r u) -> p g r u", g=2, u=2),
+                out=x_grouped[i][:, b * (K // 2) : (b + 1) * (K // 2)].bitcast(F32).rearrange("p (g r u) -> p g r u", g=2, u=2),
                 in_=xt_bank[i, b][:].rearrange("p g u r -> p g r u"),
             )
 
-        def quantise_x(i, b):
-            x_codes[i, b] = work.tile([P, 2 * P], U32, name="xc", tag="xc", bufs=6, align_bytes=64)
-            x_plane[i, b] = work.tile([P, 2 * P], U8, name="xs", tag="xs", bufs=6, align_bytes=64)
-            nc.vector.quantize_mx(out=x_codes[i, b][:].bitcast(FP8X4), scales=x_plane[i, b][:], in_=x_grouped[i, b][:])
+        def quantise_x(i, passes=slice(0, PASSES)):
+            if passes.start == 0:
+                x_codes[i] = work.tile([P, PASSES * P], U32, name="xc", tag="xc", align_bytes=64)
+                x_plane[i] = work.tile([P, PASSES * P], U8, name="xs", tag="xs", align_bytes=64)
+            cols = slice(passes.start * P, passes.stop * P)
+            nc.vector.quantize_mx(
+                out=x_codes[i][:, cols].bitcast(FP8X4),
+                scales=x_plane[i][:, cols],
+                in_=x_grouped[i][:, 4 * cols.start : 4 * cols.stop],
+            )
 
         def mx_pass(i, h, g):
             if g == 0:
                 acc[i, h] = psum.tile([P, HALF], F32, name="acc", tag="acc", bufs=4)
-            cols = slice((g % 2) * P, (g % 2 + 1) * P)
+            cols = slice(g * P, (g + 1) * P)
             nc.tensor.matmul_mx(
                 out=acc[i, h][:],
-                lhsT=x_codes[i, g // 2][:, cols].bitcast(FP8X4),
-                lhsT_scale=x_plane[i, g // 2][:, cols],
+                lhsT=x_codes[i][:, cols].bitcast(FP8X4),
+                lhsT_scale=x_plane[i][:, cols],
                 rhs=w_sb[g // 2][:, g % 2, 2 * h * HALF : 2 * (h + 1) * HALF].bitcast(FP4X4),
                 rhs_scale=w_plane[:, g, h * HALF : (h + 1) * HALF],
                 start=(g == 0),
@@ -190,15 +189,16 @@ def tile_bandpass_rectified_vibration_g4_kernel(tc, x, w_words, w_scales, c, d, 
             )
 
         def rectify(i, h, part=slice(0, HALF)):
-            if part.start == 0:
-                mag[i, h] = work.tile([P, HALF], F32, name="mag", tag="mag")
-            nc.scalar.activation(out=mag[i, h][:, part], in_=z[i, h][:, part], func=ACT.Abs)
-
-        def weigh(i, h, part=slice(0, HALF)):
             if h == 0 and part.start == 0:
-                y[i] = work.tile([P, N], F32, name="y", tag="y", bufs=6)
-            cols = slice(h * HALF + part.start, h * HALF + part.stop)
-            nc.vector.tensor_tensor(out=y[i][:, cols], in0=mag[i, h][:, part], in1=e_sb[:, cols], op=ALU.mult)
+                mag[i] = work.tile([P, N], F32, name="mag", tag="mag")
+            nc.scalar.activation(
+                out=mag[i][:, h * HALF + part.start : h * HALF + part.stop], in_=z[i, h][:, part], func=ACT.Abs
+            )
+
+        def weigh(i, cols, engine):
+            if cols.start == 0:
+                y[i] = work.tile([P, N], F32, name="y", tag="y", bufs=8)
+            engine.tensor_tensor(out=y[i][:, cols], in0=mag[i][:, cols], in1=e_sb[:, cols], op=ALU.mult)
 
         def store_y(i, cols):
             nc.sync.dma_start(out=tile_rows(y_flat, i)[:, cols], in_=y[i][:, cols])
@@ -238,8 +238,7 @@ def tile_bandpass_rectified_vibration_g4_kernel(tc, x, w_words, w_scales, c, d, 
                 scales=plane[:, h, own.start - scale_span.start : own.stop - scale_span.start],
                 in_=y_grouped[q, h][:],
             )
-            if h == 1 and codes_done:
-                nc.sync.dma_start(out=y_words32[:, :, code_span], in_=codes[:].bitcast(I32))
+            nc.sync.dma_start(out=y_words32[:, h, code_span], in_=codes[:, h, :].bitcast(I32))
             if h == 1 and scales_done:
                 for quad in range(4):
                     queue = nc.scalar if q == len(GROUP_SIZES) - 1 and quad % 2 == 0 else nc.sync
@@ -256,93 +255,78 @@ def tile_bandpass_rectified_vibration_g4_kernel(tc, x, w_words, w_scales, c, d, 
         transpose_x(0)
         copy_x(0, 0, scopy)
         copy_x(0, 1, vcopy)
-        quantise_x(0, 0)
-        spread_matmul(0)
-        spread_matmul(1)
+        quantise_x(0, slice(0, 2))
+        spread_matmul(0, "yt", 2)
+        spread_matmul(3, "yt", 2)
+        spread_matmul(1, "acc", 4)
+        spread_matmul(2, "acc", 4)
         scopy(out=d_sb[0][:], in_=spread_bank[0][:])
-        quantise_x(0, 1)
-        vcopy(out=e_sb[:], in_=spread_bank[1][:])
+        quantise_x(0, slice(2, 4))
+        vcopy(out=e_sb[:], in_=spread_bank[3][:])
+        scopy(out=d_sb[1][:], in_=spread_bank[1][:])
+        vcopy(out=d_sb[2][:], in_=spread_bank[2][:])
         for g in range(2):
             for h in range(2):
                 mx_pass(0, h, g)
+        transpose_x(1)
+        copy_x(1, 0, scopy)
+        copy_x(1, 1, vcopy)
+        for h in range(2):
+            for g in range(2, PASSES):
+                mx_pass(0, h, g)
+        quantise_x(1)
+        calibrate(0, 0)
+        rectify(0, 0)
 
         last = TILES - 1
-        unit_at = {first_tile[q] + w0 + count + 1: n for n, (q, w0, count) in enumerate(units)}
-        for i in range(TILES):
-            nxt, prev = i + 1, i - 1
-            if nxt <= last:
-                transpose_x(nxt)
-            if prev >= 0:
-                calibrate(prev, 1)
-                weigh(prev, 0)
-            if nxt <= last:
-                copy_x(nxt, 0, scopy)
-            if prev >= 0:
-                rectify(prev, 1)
-            if nxt <= last:
-                copy_x(nxt, 1, scopy)
-                quantise_x(nxt, 0)
-            if prev >= 0:
-                round_y(prev, 0, vcopy)
-                weigh(prev, 1)
-                store_y(prev, slice(0, N))
-            if nxt <= last:
-                quantise_x(nxt, 1)
-            copied = []
-            if i in unit_at:
-                transpose_y(unit_at[i], 0, "yt")
-                transpose_y(unit_at[i], 1, "yt")
-                copied = [(unit_at[i], 0)] + ([(unit_at[i], 1)] if i == last else [])
-            elif prev in unit_at:
-                copied = [(unit_at[prev], 1)]
-            for unit, h in copied:
-                copy_y(unit, h, scopy)
-            if prev >= 0:
-                round_y(prev, 1, scopy)
-            if i == 0:
-                for h in range(2):
-                    for g in range(2, PASSES):
-                        mx_pass(i, h, g)
-            else:
-                for h in range(2):
-                    for g in range(PASSES):
-                        mx_pass(i, h, g)
-            if i == last:
-                break
+        halves = [slice(0, HALF), slice(HALF, N)]
+        for i in range(1, TILES):
+            unit, h = divmod(i - 3, 2)
+            if i < last:
+                transpose_x(i + 1)
+            if i >= 3:
+                transpose_y(unit, h, "yt")
+            weigh(i - 1, halves[0], nc.gpsimd)
+            calibrate(i - 1, 1)
+            rectify(i - 1, 1)
+            weigh(i - 1, halves[1], nc.gpsimd)
+            store_y(i - 1, slice(0, N))
+            if i < last:
+                copy_x(i + 1, 0, vcopy)
+                copy_x(i + 1, 1, scopy)
+            if i >= 3:
+                copy_y(unit, h, vcopy)
+            round_y(i - 1, 0, scopy)
+            for half in range(2):
+                for g in range(PASSES):
+                    mx_pass(i, half, g)
             calibrate(i, 0)
             rectify(i, 0)
-            for unit, h in copied:
-                q, w0, count = units[unit]
-                if w0 + count == GROUP_SIZES[q]:
-                    quantise_y(q, h)
+            round_y(i - 1, 1, scopy)
+            if i < last:
+                quantise_x(i + 1)
+            if i >= 3 and unit % 2 == 1:
+                quantise_y(unit // 2, h)
 
-        groups = len(GROUP_SIZES)
         lo, hi = slice(0, HALF // 2), slice(HALF // 2, HALF)
-        calibrate(last, 0)
-        rectify(last, 0)
-        quantise_y(groups - 3, 0)
-        transpose_y(len(units) - 2, 0, "xt")
-        transpose_y(len(units) - 2, 1, "xt")
+        unit, q = len(units) - 1, len(GROUP_SIZES) - 1
+        transpose_y(unit - 1, 1, "xt")
+        weigh(last, halves[0], nc.gpsimd)
+        store_y(last, halves[0])
         calibrate(last, 1, lo)
         calibrate(last, 1, hi)
         rectify(last, 1, lo)
         rectify(last, 1, hi)
-        weigh(last, 0)
-        store_y(last, slice(0, HALF))
+        copy_y(unit - 1, 1, vcopy)
         round_y(last, 0, scopy)
-        weigh(last, 1, lo)
-        weigh(last, 1, hi)
-        store_y(last, slice(HALF, N))
+        weigh(last, slice(HALF + lo.start, HALF + lo.stop), nc.vector)
+        weigh(last, slice(HALF + hi.start, HALF + hi.stop), nc.vector)
+        store_y(last, halves[1])
+        transpose_y(unit, 0, "yt")
         round_y(last, 1, vcopy, lo)
         round_y(last, 1, vcopy, hi)
-        transpose_y(len(units) - 1, 0, "yt")
-        transpose_y(len(units) - 1, 1, "yt")
-        copy_y(len(units) - 2, 0, scopy)
-        copy_y(len(units) - 2, 1, scopy)
-        quantise_y(groups - 3, 1)
-        quantise_y(groups - 2, 0)
-        quantise_y(groups - 2, 1)
-        copy_y(len(units) - 1, 0, scopy)
-        copy_y(len(units) - 1, 1, scopy)
-        quantise_y(groups - 1, 0)
-        quantise_y(groups - 1, 1)
+        transpose_y(unit, 1, "yt")
+        copy_y(unit, 0, scopy)
+        copy_y(unit, 1, scopy)
+        quantise_y(q, 0)
+        quantise_y(q, 1)

@@ -22,7 +22,8 @@ PASSES = K // 512
 HALF = 512
 GROUP_SIZES = [4, 4, 4]
 TILES = S
-WARM_MATMULS = 4
+WARM_MATMULS = 3
+SORT = ["", ""]
 CODE_STORES = [[0], [1], [2]]
 SCALE_STORES = [[0, 1], [2]]
 
@@ -96,18 +97,19 @@ def tile_bandpass_rectified_vibration_g4_kernel(tc, x, w_words, w_scales, c, d, 
         nc.vector.memset(warm[:].bitcast(I32), 0)
         nc.vector.memset(rows[:].bitcast(I32), 0)
         nc.vector.memset(w_plane[:].rearrange("p g n -> p (g n)").bitcast(I32), 0)
-        make_identity(nc, ident[:])
+        nc.vector.memset(ident[:], 0.0)
+        make_identity(nc, ident[:], nomemset=True)
         nc.scalar.activation(out=warm_out[:], in_=warm[:, 0:8], func=ACT.Abs)
         for b in range(2):
             nc.sync.dma_start(out=x_first[b][:], in_=tile_rows(x_flat, 0)[:, b * (K // 2) : (b + 1) * (K // 2)])
         nc.sync.dma_start(out=rows[0:S, :], in_=d)
         nc.sync.dma_start(out=rows[S : S + 1, :], in_=e.rearrange("(o n) -> o n", o=1))
-        load_w(0)
-        for quad in range(4):
+        for r in range(4):
             nc.sync.dma_start(
-                out=w_plane[32 * quad : 32 * quad + 4, :, :].bitcast(I32),
-                in_=w_scales32[:, 4 * quad : 4 * quad + 4, :].rearrange("g r n -> r g n"),
+                out=w_plane[r:P:32, :, :].bitcast(I32),
+                in_=w_scales32[:, r:16:4, :].rearrange("g q n -> q g n"),
             )
+        load_w(0)
         load_x(1)
         load_w(1)
         load_c(0)
@@ -126,7 +128,7 @@ def tile_bandpass_rectified_vibration_g4_kernel(tc, x, w_words, w_scales, c, d, 
 
         xt_bank, x_grouped, x_codes, x_plane = {}, {}, {}, {}
         acc, z, mag, y, y_bf, yt_bank = {}, {}, {}, {}, {}, {}
-        y_grouped, spread_bank = {}, {}
+        y_grouped, spread_bank, x_sorted = {}, {}, {}
 
         def spread_matmul(q, tag, bufs):
             spread_bank[q] = psum.tile([P, N], BF16, name=tag, tag=tag, bufs=bufs)
@@ -134,13 +136,25 @@ def tile_bandpass_rectified_vibration_g4_kernel(tc, x, w_words, w_scales, c, d, 
                 cols = slice(h * HALF, (h + 1) * HALF)
                 nc.tensor.matmul(spread_bank[q][:, cols], lhsT=select[:, q, :], rhs=rows[:, cols], start=True, stop=True)
 
-        def transpose_x(i, tag="xt"):
+        def sort_x(i, b):
+            if SORT[b]:
+                x_sorted[i, b] = work.tile([P, 2, 2, P], F32, name="xo", tag="xo", bufs=4)
+                engine_copy = nc.scalar.copy if SORT[b] == "s" else nc.vector.tensor_copy
+                engine_copy(
+                    out=x_sorted[i, b][:],
+                    in_=x_half(i, b).bitcast(F32).rearrange("r (g p u) -> r g u p", g=2, u=2),
+                )
+
+        def transpose_x(i):
             for b in range(2):
-                xt_bank[i, b] = psum.tile([P, 2, 2, P], F32, name=tag, tag=tag)
-                words = x_half(i, b).bitcast(F32)
+                xt_bank[i, b] = psum.tile([P, 2, 2, P], F32, name="xt", tag="xt")
+                if (i, b) in x_sorted:
+                    words = x_sorted[i, b][:]
+                else:
+                    words = x_half(i, b).bitcast(F32).rearrange("r (g p u) -> r g u p", g=2, u=2)
                 for gl in range(2):
                     for u in range(2):
-                        nc.tensor.transpose(xt_bank[i, b][:, gl, u, :], words[:, 256 * gl + u : 256 * (gl + 1) : 2], ident[:])
+                        nc.tensor.transpose(xt_bank[i, b][:, gl, u, :], words[:, gl, u, :], ident[:])
 
         def copy_x(i, b, engine_copy):
             if b == 0:
@@ -174,6 +188,10 @@ def tile_bandpass_rectified_vibration_g4_kernel(tc, x, w_words, w_scales, c, d, 
                 start=(g == 0),
                 stop=(g == PASSES - 1),
             )
+
+        def mx_half(i, h):
+            for g in range(PASSES):
+                mx_pass(i, h, g)
 
         def calibrate(i, h, part=slice(0, HALF)):
             if part.start == 0:
@@ -219,35 +237,39 @@ def tile_bandpass_rectified_vibration_g4_kernel(tc, x, w_words, w_scales, c, d, 
                 for u in range(2):
                     nc.tensor.transpose(yt_bank[unit, h][:, wl, u, :], words[:, u * P : (u + 1) * P], ident[:])
 
-        def copy_y(unit, h, engine_copy):
+        def copy_y(unit, h, engine_copy, part=slice(0, P)):
             q, w0, count = units[unit]
             size = GROUP_SIZES[q]
-            if w0 == 0:
+            if (q, h) not in y_grouped:
                 y_grouped[q, h] = work.tile([P, 4 * size * P], BF16, name="yg", tag="yg", bufs=4, align_bytes=64)
             engine_copy(
-                out=y_grouped[q, h][:].bitcast(F32).rearrange("p (r s) -> p r s", r=P)[:, :, 2 * w0 : 2 * (w0 + count)],
-                in_=yt_bank[unit, h][:].rearrange("p w u r -> p r (w u)"),
+                out=y_grouped[q, h][:].bitcast(F32).rearrange("p (r s) -> p r s", r=P)[:, part, 2 * w0 : 2 * (w0 + count)],
+                in_=yt_bank[unit, h][:].rearrange("p w u r -> p r (w u)")[:, part, :],
             )
 
-        def quantise_y(q, h):
+        def quantise_y(q, h, part=slice(0, P)):
             codes, code_span, codes_done = code_batch[q]
             plane, scale_span, scales_done = scale_batch[q]
-            own = group_span(q)
+            size = GROUP_SIZES[q]
+            own = slice(group_span(q).start + part.start * size, group_span(q).start + part.stop * size)
             nc.vector.quantize_mx(
                 out=codes[:, h, own.start - code_span.start : own.stop - code_span.start].bitcast(FP8X4),
                 scales=plane[:, h, own.start - scale_span.start : own.stop - scale_span.start],
-                in_=y_grouped[q, h][:],
+                in_=y_grouped[q, h][:, 4 * size * part.start : 4 * size * part.stop],
             )
+
+        def store_codes(q, h):
+            codes, code_span, codes_done = code_batch[q]
             nc.sync.dma_start(out=y_words32[:, h, code_span], in_=codes[:, h, :].bitcast(I32))
-            if h == 1 and scales_done:
-                for quad in range(4):
-                    queue = nc.scalar if q == len(GROUP_SIZES) - 1 and quad % 2 == 0 else nc.sync
-                    queue.dma_start(
-                        out=y_scales32[:, 4 * quad : 4 * quad + 4, scale_span.start // 4 : scale_span.stop // 4].rearrange(
-                            "g r m -> r g m"
-                        ),
-                        in_=plane[32 * quad : 32 * quad + 4, :, :].bitcast(I32),
-                    )
+
+        def store_scales(q):
+            plane, scale_span, scales_done = scale_batch[q]
+            for r in range(4):
+                queue = nc.scalar if q == len(GROUP_SIZES) - 1 and r % 2 == 0 else nc.sync
+                queue.dma_start(
+                    out=y_scales32[:, r:16:4, scale_span.start // 4 : scale_span.stop // 4].rearrange("g q m -> q g m"),
+                    in_=plane[r:P:32, :, :].bitcast(I32),
+                )
 
         vcopy = nc.vector.tensor_copy
         scopy = nc.scalar.copy
@@ -280,53 +302,56 @@ def tile_bandpass_rectified_vibration_g4_kernel(tc, x, w_words, w_scales, c, d, 
 
         last = TILES - 1
         halves = [slice(0, HALF), slice(HALF, N)]
-        for i in range(1, TILES):
+        for i in range(1, last):
             unit, h = divmod(i - 3, 2)
-            if i < last:
-                transpose_x(i + 1)
-            if i >= 3:
-                transpose_y(unit, h, "yt")
-            weigh(i - 1, halves[0], nc.gpsimd)
+            transpose_x(i + 1)
             calibrate(i - 1, 1)
+            if i >= 2: round_y(i - 2, 1, vcopy)
+            if i >= 3: transpose_y(unit, h, "yt")
+            mx_half(i, 0)
+            weigh(i - 1, halves[0], nc.vector)
             rectify(i - 1, 1)
-            weigh(i - 1, halves[1], nc.gpsimd)
-            store_y(i - 1, slice(0, N))
-            if i < last:
-                copy_x(i + 1, 0, vcopy)
-                copy_x(i + 1, 1, scopy)
-            if i >= 3:
-                copy_y(unit, h, vcopy)
-            round_y(i - 1, 0, scopy)
-            for half in range(2):
-                for g in range(PASSES):
-                    mx_pass(i, half, g)
+            weigh(i - 1, halves[1], nc.vector); store_y(i - 1, slice(0, N))
+            mx_half(i, 1)
+            copy_x(i + 1, 0, scopy)
+            copy_x(i + 1, 1, scopy)
+            if i >= 3: copy_y(unit, h, scopy)
             calibrate(i, 0)
+            round_y(i - 1, 0, scopy)
+            quantise_x(i + 1)
+            if i >= 3 and unit % 2 == 1 and i < last - 1: quantise_y(unit // 2, h); store_codes(unit // 2, h)
             rectify(i, 0)
-            round_y(i - 1, 1, scopy)
-            if i < last:
-                quantise_x(i + 1)
-            if i >= 3 and unit % 2 == 1:
-                quantise_y(unit // 2, h)
-
-        lo, hi = slice(0, HALF // 2), slice(HALF // 2, HALF)
-        unit, q = len(units) - 1, len(GROUP_SIZES) - 1
-        transpose_y(unit - 1, 1, "xt")
-        weigh(last, halves[0], nc.gpsimd)
-        store_y(last, halves[0])
-        calibrate(last, 1, lo)
-        calibrate(last, 1, hi)
-        rectify(last, 1, lo)
-        rectify(last, 1, hi)
-        copy_y(unit - 1, 1, vcopy)
-        round_y(last, 0, scopy)
-        weigh(last, slice(HALF + lo.start, HALF + lo.stop), nc.vector)
-        weigh(last, slice(HALF + hi.start, HALF + hi.stop), nc.vector)
-        store_y(last, halves[1])
-        transpose_y(unit, 0, "yt")
-        round_y(last, 1, vcopy, lo)
-        round_y(last, 1, vcopy, hi)
-        transpose_y(unit, 1, "yt")
-        copy_y(unit, 0, scopy)
-        copy_y(unit, 1, scopy)
-        quantise_y(q, 0)
-        quantise_y(q, 1)
+        round_y(9, 1, vcopy)
+        calibrate(10, 1)
+        transpose_y(4, 0, "yt")
+        rectify(10, 1)
+        transpose_y(4, 1, "yt")
+        mx_half(11, 0)
+        copy_y(4, 1, scopy)
+        copy_y(4, 0, scopy)
+        quantise_y(1, 1); store_codes(1, 1); store_scales(1)
+        weigh(10, halves[0], nc.vector)
+        round_y(10, 0, scopy)
+        weigh(10, halves[1], nc.vector); store_y(10, slice(0, N))
+        calibrate(11, 0)
+        mx_half(11, 1)
+        calibrate(11, 1, slice(0, 256))
+        calibrate(11, 1, slice(256, 512))
+        rectify(11, 0)
+        rectify(11, 1, slice(0, 256))
+        weigh(11, halves[0], nc.vector); store_y(11, halves[0])
+        round_y(10, 1, vcopy)
+        weigh(11, slice(512, 768), nc.vector)
+        rectify(11, 1, slice(256, 512))
+        weigh(11, slice(768, 1024), nc.vector); store_y(11, halves[1])
+        round_y(11, 0, scopy)
+        round_y(11, 1, scopy, slice(0, 256))
+        transpose_y(5, 0, "xt")
+        copy_y(5, 0, scopy)
+        round_y(11, 1, vcopy, slice(256, 512))
+        transpose_y(5, 1, "xt")
+        copy_y(5, 1, scopy, slice(0, 64))
+        quantise_y(2, 0); store_codes(2, 0)
+        copy_y(5, 1, scopy, slice(64, 128))
+        quantise_y(2, 1, slice(0, 64))
+        quantise_y(2, 1, slice(64, 128)); store_codes(2, 1); store_scales(2)

@@ -25,7 +25,7 @@ TILES = S
 WARM_MATMULS = 3
 SORT = ["", ""]
 CODE_STORES = [[0], [1], [2]]
-SCALE_STORES = [[0, 1], [2]]
+SCALE_STORES = [[0], [1], [2]]
 
 
 def tile_bandpass_rectified_vibration_g4_kernel(tc, x, w_words, w_scales, c, d, e, out_0, out_1, out_2):
@@ -94,10 +94,10 @@ def tile_bandpass_rectified_vibration_g4_kernel(tc, x, w_words, w_scales, c, d, 
             nc.sync.dma_start(out=c_sb[q][:], in_=c_flat[group_span(q)].rearrange("(p w) -> p w", p=P))
 
         size0 = GROUP_SIZES[0]
+        nc.vector.memset(ident[:], 0.0)
         nc.vector.memset(warm[:].bitcast(I32), 0)
         nc.vector.memset(rows[:].bitcast(I32), 0)
         nc.vector.memset(w_plane[:].rearrange("p g n -> p (g n)").bitcast(I32), 0)
-        nc.vector.memset(ident[:], 0.0)
         make_identity(nc, ident[:], nomemset=True)
         nc.scalar.activation(out=warm_out[:], in_=warm[:, 0:8], func=ACT.Abs)
         for b in range(2):
@@ -136,10 +136,9 @@ def tile_bandpass_rectified_vibration_g4_kernel(tc, x, w_words, w_scales, c, d, 
                 cols = slice(h * HALF, (h + 1) * HALF)
                 nc.tensor.matmul(spread_bank[q][:, cols], lhsT=select[:, q, :], rhs=rows[:, cols], start=True, stop=True)
 
-        def sort_x(i, b):
-            if SORT[b]:
+        def sort_x(i, b, engine_copy):
+            if engine_copy and i < TILES:
                 x_sorted[i, b] = work.tile([P, 2, 2, P], F32, name="xo", tag="xo", bufs=4)
-                engine_copy = nc.scalar.copy if SORT[b] == "s" else nc.vector.tensor_copy
                 engine_copy(
                     out=x_sorted[i, b][:],
                     in_=x_half(i, b).bitcast(F32).rearrange("r (g p u) -> r g u p", g=2, u=2),
@@ -258,9 +257,10 @@ def tile_bandpass_rectified_vibration_g4_kernel(tc, x, w_words, w_scales, c, d, 
                 in_=y_grouped[q, h][:, 4 * size * part.start : 4 * size * part.stop],
             )
 
-        def store_codes(q, h):
+        def store_codes(q, h, part=slice(0, P)):
             codes, code_span, codes_done = code_batch[q]
-            nc.sync.dma_start(out=y_words32[:, h, code_span], in_=codes[:, h, :].bitcast(I32))
+            cols = slice(part.start * GROUP_SIZES[q], part.stop * GROUP_SIZES[q])
+            nc.sync.dma_start(out=y_words32[:, h, code_span][:, cols], in_=codes[:, h, cols].bitcast(I32))
 
         def store_scales(q):
             plane, scale_span, scales_done = scale_batch[q]
@@ -319,7 +319,11 @@ def tile_bandpass_rectified_vibration_g4_kernel(tc, x, w_words, w_scales, c, d, 
             calibrate(i, 0)
             round_y(i - 1, 0, scopy)
             quantise_x(i + 1)
-            if i >= 3 and unit % 2 == 1 and i < last - 1: quantise_y(unit // 2, h); store_codes(unit // 2, h)
+            if i >= 3 and unit % 2 == 1 and i < last - 1:
+                quantise_y(unit // 2, h)
+                store_codes(unit // 2, h)
+                if h == 1:
+                    store_scales(unit // 2)
             rectify(i, 0)
         round_y(9, 1, vcopy)
         calibrate(10, 1)
@@ -354,4 +358,7 @@ def tile_bandpass_rectified_vibration_g4_kernel(tc, x, w_words, w_scales, c, d, 
         quantise_y(2, 0); store_codes(2, 0)
         copy_y(5, 1, scopy, slice(64, 128))
         quantise_y(2, 1, slice(0, 64))
-        quantise_y(2, 1, slice(64, 128)); store_codes(2, 1); store_scales(2)
+        store_codes(2, 1, slice(0, 64))
+        quantise_y(2, 1, slice(64, 128))
+        store_codes(2, 1, slice(64, 128))
+        store_scales(2)

from contextlib import ExitStack

import concourse.mybir as mybir
from concourse.masks import make_identity

S, V, K, N = 12, 128, 2048, 1024
M = S * V
FLOPS = 2 * M * K * N

F32 = mybir.dt.float32
BF16 = mybir.dt.bfloat16
I32 = mybir.dt.int32
U32 = mybir.dt.uint32
U8 = mybir.dt.uint8
FP8X4 = mybir.dt.float8_e4m3fn_x4
FP4X4 = mybir.dt.float4_e2m1fn_x4
ALU = mybir.AluOpType
ACT = mybir.ActivationFunctionType

P = 128
PASSES = K // 512
HALF = 512
GROUP_SIZES = [4, 4, 4]
TILES = S
WARM_MATMULS = 3
SORT = ["", ""]
CODE_STORES = [[0], [1], [2]]
SCALE_STORES = [[0], [1], [2]]


def tile_bandpass_rectified_vibration_g4_kernel(tc, x, w_words, w_scales, c, d, e, out_0, out_1, out_2):
    nc = tc.nc
    x_flat = x.rearrange("a v k -> (a v) k")
    y_flat = out_0.rearrange("a v n -> (a v) n")
    c_flat = c.rearrange("a v -> (a v)")
    first_tile = [sum(GROUP_SIZES[:q]) for q in range(len(GROUP_SIZES))]
    place = [(q, w) for q, size in enumerate(GROUP_SIZES) for w in range(size)]
    units = [(q, w, min(2, size)) for q, size in enumerate(GROUP_SIZES) for w in range(0, size, 2)]

    def group_span(q):
        return slice(first_tile[q] * P, (first_tile[q] + GROUP_SIZES[q]) * P)

    def tile_rows(flat, i):
        q, w = place[i]
        return flat[group_span(q), :].rearrange("(p w) n -> w p n", p=P)[w]

    w_words32 = w_words.bitcast(I32).rearrange("g p n -> p g n")
    w_scales32 = w_scales.bitcast(I32)
    y_words32 = out_1.rearrange("g p m t -> g p (m t)").bitcast(I32).rearrange("g p m -> p g m")
    y_scales32 = out_2.bitcast(I32)

    with ExitStack() as ctx:
        keep = ctx.enter_context(tc.tile_pool(name="keep", bufs=1))
        work = ctx.enter_context(tc.tile_pool(name="work", bufs=3))
        psum = ctx.enter_context(tc.psum_pool(name="psum", bufs=2))
        ctx.enter_context(tc.manual_schedule())

        ident = keep.tile([P, P], F32)
        select = keep.tile([P, len(GROUP_SIZES) + 1, P], BF16)
        rows = keep.tile([P, N], BF16)
        d_sb = [keep.tile([P, N], BF16, name="d%d" % q) for q in range(len(GROUP_SIZES))]
        e_sb = keep.tile([P, N], BF16)
        c_sb = [keep.tile([P, size], BF16, name="c%d" % q) for q, size in enumerate(GROUP_SIZES)]
        w_sb = [keep.tile([P, 2, 2 * N], U8, name="w%d" % b, align_bytes=64) for b in range(2)]
        w_plane = keep.tile([P, PASSES, N], U8, align_bytes=64)
        code_batch, scale_batch = {}, {}
        for n, members in enumerate(CODE_STORES):
            span = slice(group_span(members[0]).start, group_span(members[-1]).stop)
            codes = keep.tile([P, 2, span.stop - span.start], U32, name="yc%d" % n, align_bytes=64)
            for q in members:
                code_batch[q] = (codes, span, q == members[-1])
        for n, members in enumerate(SCALE_STORES):
            span = slice(group_span(members[0]).start, group_span(members[-1]).stop)
            plane = keep.tile([P, 2, span.stop - span.start], U8, name="ys%d" % n, align_bytes=64)
            for q in members:
                scale_batch[q] = (plane, span, q == members[-1])
        warm = keep.tile([P, HALF], BF16)
        warm_out = keep.tile([P, 8], F32)
        x_first = [keep.tile([P, K // 2], BF16, name="x0_%d" % b) for b in range(2)]
        x_rest = [keep.tile([P, K], BF16, name="x%d" % i) for i in range(1, TILES)]

        def x_half(i, b):
            if i == 0:
                return x_first[b][:]
            return x_rest[i - 1][:, b * (K // 2) : (b + 1) * (K // 2)]

        def load_x(i):
            nc.sync.dma_start(out=x_rest[i - 1][:], in_=tile_rows(x_flat, i))

        def load_w(b):
            nc.sync.dma_start(out=w_sb[b][:].bitcast(I32), in_=w_words32[:, 2 * b : 2 * b + 2, :])

        def load_c(q):
            nc.sync.dma_start(out=c_sb[q][:], in_=c_flat[group_span(q)].rearrange("(p w) -> p w", p=P))

        size0 = GROUP_SIZES[0]
        nc.vector.memset(ident[:], 0.0)
        nc.vector.memset(warm[:].bitcast(I32), 0)
        nc.vector.memset(rows[:].bitcast(I32), 0)
        nc.vector.memset(w_plane[:].rearrange("p g n -> p (g n)").bitcast(I32), 0)
        make_identity(nc, ident[:], nomemset=True)
        nc.scalar.activation(out=warm_out[:], in_=warm[:, 0:8], func=ACT.Abs)
        for b in range(2):
            nc.sync.dma_start(out=x_first[b][:], in_=tile_rows(x_flat, 0)[:, b * (K // 2) : (b + 1) * (K // 2)])
        nc.sync.dma_start(out=rows[0:S, :], in_=d)
        nc.sync.dma_start(out=rows[S : S + 1, :], in_=e.rearrange("(o n) -> o n", o=1))
        for r in range(4):
            nc.sync.dma_start(
                out=w_plane[r:P:32, :, :].bitcast(I32),
                in_=w_scales32[:, r:16:4, :].rearrange("g q n -> q g n"),
            )
        load_w(0)
        load_x(1)
        load_w(1)
        load_c(0)
        for i in range(2, TILES):
            load_x(i)
            if i + 1 in first_tile:
                load_c(place[i + 1][0])
        nc.vector.tensor_copy(
            out=select[:, 0:3, :].rearrange("k q (a j) -> k (q a) j", a=size0),
            in_=ident[:, 0:S].unsqueeze(2).to_broadcast([P, S, P // size0]),
        )
        nc.vector.tensor_copy(out=select[:, 3, :], in_=ident[:, S : S + 1].to_broadcast([P, P]))
        warm_bank = psum.tile([P, HALF], F32, name="acc", tag="acc", bufs=4)
        for j in range(WARM_MATMULS):
            nc.tensor.matmul(warm_bank[:], lhsT=warm[:, 0:P], rhs=warm[:], start=True, stop=True)

        xt_bank, x_grouped, x_codes, x_plane = {}, {}, {}, {}
        acc, z, mag, y, y_bf, yt_bank = {}, {}, {}, {}, {}, {}
        y_grouped, spread_bank, x_sorted = {}, {}, {}

        def spread_matmul(q, tag, bufs):
            spread_bank[q] = psum.tile([P, N], BF16, name=tag, tag=tag, bufs=bufs)
            for h in range(2):
                cols = slice(h * HALF, (h + 1) * HALF)
                nc.tensor.matmul(spread_bank[q][:, cols], lhsT=select[:, q, :], rhs=rows[:, cols], start=True, stop=True)

        def sort_x(i, b, engine_copy):
            if engine_copy and i < TILES:
                x_sorted[i, b] = work.tile([P, 2, 2, P], F32, name="xo", tag="xo", bufs=4)
                engine_copy(
                    out=x_sorted[i, b][:],
                    in_=x_half(i, b).bitcast(F32).rearrange("r (g p u) -> r g u p", g=2, u=2),
                )

        def transpose_x(i):
            for b in range(2):
                xt_bank[i, b] = psum.tile([P, 2, 2, P], F32, name="xt", tag="xt")
                if (i, b) in x_sorted:
                    words = x_sorted[i, b][:]
                else:
                    words = x_half(i, b).bitcast(F32).rearrange("r (g p u) -> r g u p", g=2, u=2)
                for gl in range(2):
                    for u in range(2):
                        nc.tensor.transpose(xt_bank[i, b][:, gl, u, :], words[:, gl, u, :], ident[:])

        def copy_x(i, b, engine_copy):
            if b == 0:
                x_grouped[i] = work.tile([P, K], BF16, name="xg", tag="xg", align_bytes=64)
            engine_copy(
                out=x_grouped[i][:, b * (K // 2) : (b + 1) * (K // 2)].bitcast(F32).rearrange("p (g r u) -> p g r u", g=2, u=2),
                in_=xt_bank[i, b][:].rearrange("p g u r -> p g r u"),
            )

        def quantise_x(i, passes=slice(0, PASSES)):
            if passes.start == 0:
                x_codes[i] = work.tile([P, PASSES * P], U32, name="xc", tag="xc", align_bytes=64)
                x_plane[i] = work.tile([P, PASSES * P], U8, name="xs", tag="xs", align_bytes=64)
            cols = slice(passes.start * P, passes.stop * P)
            nc.vector.quantize_mx(
                out=x_codes[i][:, cols].bitcast(FP8X4),
                scales=x_plane[i][:, cols],
                in_=x_grouped[i][:, 4 * cols.start : 4 * cols.stop],
            )

        def mx_pass(i, h, g):
            if g == 0:
                acc[i, h] = psum.tile([P, HALF], F32, name="acc", tag="acc", bufs=4)
            cols = slice(g * P, (g + 1) * P)
            nc.tensor.matmul_mx(
                out=acc[i, h][:],
                lhsT=x_codes[i][:, cols].bitcast(FP8X4),
                lhsT_scale=x_plane[i][:, cols],
                rhs=w_sb[g // 2][:, g % 2, 2 * h * HALF : 2 * (h + 1) * HALF].bitcast(FP4X4),
                rhs_scale=w_plane[:, g, h * HALF : (h + 1) * HALF],
                start=(g == 0),
                stop=(g == PASSES - 1),
            )

        def mx_half(i, h):
            for g in range(PASSES):
                mx_pass(i, h, g)

        def calibrate(i, h, part=slice(0, HALF)):
            if part.start == 0:
                z[i, h] = work.tile([P, HALF], F32, name="z", tag="z")
            q, w = place[i]
            nc.vector.scalar_tensor_tensor(
                out=z[i, h][:, part],
                in0=acc[i, h][:, part],
                scalar=c_sb[q][:, w : w + 1],
                in1=d_sb[q][:, h * HALF + part.start : h * HALF + part.stop],
                op0=ALU.mult,
                op1=ALU.subtract,
            )

        def rectify(i, h, part=slice(0, HALF)):
            if h == 0 and part.start == 0:
                mag[i] = work.tile([P, N], F32, name="mag", tag="mag")
            nc.scalar.activation(
                out=mag[i][:, h * HALF + part.start : h * HALF + part.stop], in_=z[i, h][:, part], func=ACT.Abs
            )

        def weigh(i, cols, engine):
            if cols.start == 0:
                y[i] = work.tile([P, N], F32, name="y", tag="y", bufs=8)
            engine.tensor_tensor(out=y[i][:, cols], in0=mag[i][:, cols], in1=e_sb[:, cols], op=ALU.mult)

        def store_y(i, cols):
            nc.sync.dma_start(out=tile_rows(y_flat, i)[:, cols], in_=y[i][:, cols])

        def round_y(i, h, engine_copy, part=slice(0, HALF)):
            if part.start == 0:
                y_bf[i, h] = work.tile([P, HALF], BF16, name="ybf", tag="ybf", bufs=8)
            engine_copy(
                out=y_bf[i, h][:].rearrange("r (u p e) -> r u p e", u=2, e=2)[:, :, part.start // 4 : part.stop // 4, :],
                in_=y[i][:, h * HALF + part.start : h * HALF + part.stop].rearrange("r (p u e) -> r u p e", u=2, e=2),
            )

        def transpose_y(unit, h, tag):
            q, w0, count = units[unit]
            yt_bank[unit, h] = psum.tile([P, count, 2, P], F32, name=tag, tag=tag)
            for wl in range(count):
                words = y_bf[first_tile[q] + w0 + wl, h][:].bitcast(F32)
                for u in range(2):
                    nc.tensor.transpose(yt_bank[unit, h][:, wl, u, :], words[:, u * P : (u + 1) * P], ident[:])

        def copy_y(unit, h, engine_copy, part=slice(0, P)):
            q, w0, count = units[unit]
            size = GROUP_SIZES[q]
            if (q, h) not in y_grouped:
                y_grouped[q, h] = work.tile([P, 4 * size * P], BF16, name="yg", tag="yg", bufs=4, align_bytes=64)
            engine_copy(
                out=y_grouped[q, h][:].bitcast(F32).rearrange("p (r s) -> p r s", r=P)[:, part, 2 * w0 : 2 * (w0 + count)],
                in_=yt_bank[unit, h][:].rearrange("p w u r -> p r (w u)")[:, part, :],
            )

        def quantise_y(q, h, part=slice(0, P)):
            codes, code_span, codes_done = code_batch[q]
            plane, scale_span, scales_done = scale_batch[q]
            size = GROUP_SIZES[q]
            own = slice(group_span(q).start + part.start * size, group_span(q).start + part.stop * size)
            nc.vector.quantize_mx(
                out=codes[:, h, own.start - code_span.start : own.stop - code_span.start].bitcast(FP8X4),
                scales=plane[:, h, own.start - scale_span.start : own.stop - scale_span.start],
                in_=y_grouped[q, h][:, 4 * size * part.start : 4 * size * part.stop],
            )

        def store_codes(q, h, part=slice(0, P)):
            codes, code_span, codes_done = code_batch[q]
            cols = slice(part.start * GROUP_SIZES[q], part.stop * GROUP_SIZES[q])
            nc.sync.dma_start(out=y_words32[:, h, code_span][:, cols], in_=codes[:, h, cols].bitcast(I32))

        def store_scales(q):
            plane, scale_span, scales_done = scale_batch[q]
            for r in range(4):
                queue = nc.scalar if q == len(GROUP_SIZES) - 1 and r % 2 == 0 else nc.sync
                queue.dma_start(
                    out=y_scales32[:, r:16:4, scale_span.start // 4 : scale_span.stop // 4].rearrange("g q m -> q g m"),
                    in_=plane[r:P:32, :, :].bitcast(I32),
                )

        vcopy = nc.vector.tensor_copy
        scopy = nc.scalar.copy

        transpose_x(0)
        copy_x(0, 0, scopy)
        copy_x(0, 1, vcopy)
        quantise_x(0, slice(0, 2))
        spread_matmul(0, "yt", 2)
        spread_matmul(3, "yt", 2)
        spread_matmul(1, "acc", 4)
        spread_matmul(2, "acc", 4)
        scopy(out=d_sb[0][:], in_=spread_bank[0][:])
        quantise_x(0, slice(2, 4))
        vcopy(out=e_sb[:], in_=spread_bank[3][:])
        scopy(out=d_sb[1][:], in_=spread_bank[1][:])
        vcopy(out=d_sb[2][:], in_=spread_bank[2][:])
        for g in range(2):
            for h in range(2):
                mx_pass(0, h, g)
        transpose_x(1)
        copy_x(1, 0, scopy)
        copy_x(1, 1, vcopy)
        for h in range(2):
            for g in range(2, PASSES):
                mx_pass(0, h, g)
        quantise_x(1)
        calibrate(0, 0)
        rectify(0, 0)

        last = TILES - 1
        halves = [slice(0, HALF), slice(HALF, N)]
        for i in range(1, last):
            unit, h = divmod(i - 3, 2)
            transpose_x(i + 1)
            calibrate(i - 1, 1)
            if i >= 2: round_y(i - 2, 1, vcopy)
            if i >= 3: transpose_y(unit, h, "yt")
            mx_half(i, 0)
            weigh(i - 1, halves[0], nc.vector)
            rectify(i - 1, 1)
            weigh(i - 1, halves[1], nc.vector); store_y(i - 1, slice(0, N))
            mx_half(i, 1)
            copy_x(i + 1, 0, scopy)
            copy_x(i + 1, 1, scopy)
            if i >= 3: copy_y(unit, h, scopy)
            calibrate(i, 0)
            round_y(i - 1, 0, scopy)
            quantise_x(i + 1)
            if i >= 3 and unit % 2 == 1 and i < last - 1:
                quantise_y(unit // 2, h)
                store_codes(unit // 2, h)
                if h == 1:
                    store_scales(unit // 2)
            rectify(i, 0)
        round_y(9, 1, vcopy)
        calibrate(10, 1)
        transpose_y(4, 0, "yt")
        rectify(10, 1)
        transpose_y(4, 1, "yt")
        mx_half(11, 0)
        copy_y(4, 1, scopy)
        copy_y(4, 0, scopy)
        quantise_y(1, 1); store_codes(1, 1); store_scales(1)
        weigh(10, halves[0], nc.vector)
        round_y(10, 0, scopy)
        weigh(10, halves[1], nc.vector); store_y(10, slice(0, N))
        calibrate(11, 0)
        mx_half(11, 1)
        calibrate(11, 1, slice(0, 256))
        calibrate(11, 1, slice(256, 512))
        rectify(11, 0)
        rectify(11, 1, slice(0, 256))
        weigh(11, halves[0], nc.vector); store_y(11, halves[0])
        round_y(10, 1, vcopy)
        weigh(11, slice(512, 768), nc.vector)
        rectify(11, 1, slice(256, 512))
        weigh(11, slice(768, 1024), nc.vector); store_y(11, halves[1])
        round_y(11, 0, scopy)
        round_y(11, 1, scopy, slice(0, 256))
        transpose_y(5, 0, "xt")
        copy_y(5, 0, scopy)
        round_y(11, 1, vcopy, slice(256, 512))
        transpose_y(5, 1, "xt")
        copy_y(5, 1, scopy, slice(0, 64))
        quantise_y(2, 0); store_codes(2, 0)
        copy_y(5, 1, scopy, slice(64, 128))
        quantise_y(2, 1, slice(0, 64))
        store_codes(2, 1, slice(0, 64))
        quantise_y(2, 1, slice(64, 128))
        store_codes(2, 1, slice(64, 128))
        store_scales(2)
